import numpy as np, ml_dtypes
CORES = [113,118,241,246]
N = 4
BF = ml_dtypes.bfloat16
def gentries(a):
    return np.ascontiguousarray(a.reshape(8, 16, -1).transpose(0, 2, 1)).reshape(8, -1)
def gtable(e):
    e = np.asarray(e); return np.ascontiguousarray(e.reshape(8, -1, 16).transpose(0, 2, 1)).reshape(128, -1).astype(np.int32)
S, R, B, C, P, STEPS, O = 1568, 1568, 160, 3, 3, 2, 480
def pick(t, l):
    return np.stack([np.stack([np.take(t[r, g], l[r, g], axis=1) for g in range(8)]) for r in range(N)])
def widen(t, send):
    s = pick(t, send)
    return np.stack([np.concatenate([t[r]] + [s[(r + 1 + m) % N][:, :, (N - 2 - m) * B:(N - 1 - m) * B] for m in range(N - 1)], axis=2) for r in range(N)])
def groups(a):
    return np.stack([gentries(v) for v in a])
def first(v):
    u, i, n = np.unique(v, return_index=True, return_inverse=True); return i[n.reshape(-1)]
def network(rng, pairs):
    reac = np.zeros((N, 8, 2 * R), np.int64); cons = np.full((N, 8, C * S), R + O); sp = np.zeros((N, 8, O), np.int64); rx = np.zeros((N, 8, O), np.int64)
    for g in range(8):
        inc, use = [], []
        for r in range(N):
            if pairs:
                inc.append((rng.permutation(R)[:, None] + R * np.arange(2)).reshape(-1)); use.append((rng.permutation(S)[:, None] + S * np.arange(C)).reshape(-1)[:2 * R])
            else:
                inc.append(rng.permutation(2 * R)); use.append(rng.permutation(C * S)[:2 * R])
            e, u = inc[r], use[r]
            rx[r, g] = e[:O] % R; sp[r, g] = u[:O] % S
            reac[r, g, e[O:]] = u[O:] % S; cons[r, g, u[O:]] = e[O:] % R
        for r in range(N):
            for m in range(N - 1):
                q, k = (r + 1 + m) % N, N - 2 - m
                e = inc[r][m * B:(m + 1) * B]; u = use[q][k * B:(k + 1) * B]; n = np.arange(B); j = n if pairs else rng.permutation(B)
                reac[r, g, e] = S + m * B + (first(u % S) if pairs else j)
                cons[q, g, u[j]] = R + k * B + (first(e % R) if pairs else n)
    prod = rng.integers(0, R + O, (N, 8, P * S)); prod[rng.random(prod.shape) < 0.25] = R + O
    return reac, cons, prod, sp, rx
def pack(x, rate, net):
    return dict([("x", np.ascontiguousarray(np.reshape(x, (N, 128, S))).astype(np.int32)), ("rate", rate.astype(np.int32))] + [(n, np.stack([gtable(e) for e in v])) for n, v in zip(("reac", "cons", "prod", "spsend", "rxsend"), net)])
def some(rng):
    return rng.integers(0, 256, (N, 8, 16, S)) >> rng.integers(0, 8, (N, 8, 16, S)), rng.integers(1, 128, (N, 8, R)) >> rng.integers(0, 4, (N, 8, R))
def setup_inputs(rng):
    net = network(rng, False); x, k = some(rng); return pack(x, k, net)
def setup_inputs_ties(rng):
    net = network(rng, False); n = np.sum(net[1].reshape(N, 8, C, S) != R + O, axis=2)[:, :, None]
    x = np.where(n < 2, 5 + rng.integers(0, 4, (N, 8, 16, S)), 3 * n - rng.integers(0, 2, (N, 8, 16, S)))
    return pack(x, rng.integers(123, 128, (N, 8, R)), net)
def setup_inputs_twins(rng):
    net = network(rng, True); x, k = some(rng); return pack(x, k, net)
def setup_inputs_ends(rng):
    net = network(rng, False); p = rng.choice(np.array([0, R - 1, R, R + O - 1, R + O]), (N, 8, P * S))
    x = 255 * (rng.random((N, 8, 16, S)) < 0.9); k = 127 * (rng.random((N, 8, R)) < 0.9)
    return pack(x, k, net[:2] + (p,) + net[3:])
def setup_inputs_spread(rng):
    net = network(rng, False); w = rng.random((N, 8, 1, S)); x = rng.integers(0, 256, (N, 8, 16, S))
    x = np.where(w < 0.05, 0, np.where(w < 0.15, 255, np.where(w < 0.5, x, x >> 5)))
    w = rng.random((N, 8, R)); k = rng.integers(0, 128, (N, 8, R)); k = np.where(w < 0.05, 0, np.where(w < 0.15, 127, np.where(w < 0.5, k, k >> 4)))
    return pack(x, k, net)
def check_inputs(d):
    try:
        top = {"x": 255, "rate": 127, "reac": S + O - 1, "cons": R + O, "prod": R + O, "spsend": S - 1, "rxsend": R - 1}
        bad = [n + " range" for n in top if d[n].min() < 0 or d[n].max() > top[n]]
        if bad: return bad
        ra, co, ss, rs = groups(d["reac"]), groups(d["cons"]), groups(d["spsend"]), groups(d["rxsend"])
        ids = np.broadcast_to(np.arange(N * S, dtype=np.int64).reshape(N, 1, 1, S), (N, 8, 1, S)); idr = np.broadcast_to(np.arange(N * R, dtype=np.int64).reshape(N, 1, 1, R), (N, 8, 1, R))
        net = np.arange(8, dtype=np.int64).reshape(1, 8, 1); own = np.arange(N, dtype=np.int64).reshape(N, 1, 1)
        a = (net * (N * S) + pick(widen(ids, ss), ra)[:, :, 0]) * (N * R) + own * R + np.arange(2 * R) % R
        w = pick(np.concatenate([widen(idr, rs), np.full((N, 8, 1, 1), -1)], axis=3), co)[:, :, 0]
        b = ((net * (N * S) + own * S + np.arange(C * S) % S) * (N * R) + w)[w >= 0]
        return [] if np.array_equal(np.sort(a.reshape(-1)), np.sort(b)) else ["cons fits reac"]
    except Exception:
        return ["form"]
def reference(x, rate, reac, cons, prod, spsend, rxsend):
    n = x.astype(np.int32).reshape(N, 8, 16, S); k = rate.astype(np.int32)[:, :, None]; none = np.zeros((N, 8, 16, 1), np.int32)
    ra, co, pr, ss, rs = groups(reac), groups(cons), groups(prod), groups(spsend), groups(rxsend)
    for step in range(STEPS):
        a = pick(widen(n, ss), ra)
        f = np.minimum(3, (k * a[..., :R] * a[..., R:]) >> 10)
        w = np.concatenate([widen(f, rs), none], axis=3)
        demand = np.sum(pick(w, co).reshape(N, 8, 16, C, S), axis=3)
        veto = (demand > n).astype(np.int32)
        b = pick(widen(veto, ss), ra)
        f = f * ((b[..., :R] + b[..., R:]) == 0)
        w = np.concatenate([widen(f, rs), none], axis=3)
        n = n - np.sum(pick(w, co).reshape(N, 8, 16, C, S), axis=3) + np.sum(pick(w, pr).reshape(N, 8, 16, P, S), axis=3)
    return {"y": n.reshape(N, 128, S).astype(np.float32)}

@@ -1,0 +1,416 @@
+from concourse.bass import DstId, RemoteDMATransfer
+from concourse.mybir import AluOpType, ActivationFunctionType
+
+S = 1568
+CH = [(0, 416), (416, 384), (800, 384), (1184, 384)]
+VS = [(0, 448), (448, 448), (896, 416), (1312, 256)]
+HALF = 128.500244140625
+
+SCRATCH = {
+    "sx": ("dram", [4, 128, 392], "bfloat16"), "lx": ("dram", [4, 128, 392], "bfloat16"),
+    "se": ("dram", [4, 128, 98], "int32"), "le": ("dram", [4, 128, 98], "int32"),
+    "sl": ("dram", [4, 128, 147], "int32"), "ll": ("dram", [4, 128, 147], "int32"),
+    "E32": ("sbuf", [128, 392], "int32"), "LST": ("sbuf", [128, 392], "uint16"), "CPL": ("sbuf", [128, 588], "uint16"),
+    "IW": ("sbuf", [128, 256], "int32"), "IM": ("sbuf", [128, 16], "int32"), "IB": ("sbuf", [128, 128], "int32"),
+    "JW": ("sbuf", [128, 256], "int32"), "JM": ("sbuf", [128, 16], "int32"), "JB": ("sbuf", [128, 128], "int32"),
+    "W": ("sbuf", [128, 256], "bfloat16"), "NI": ("sbuf", [128, 128], "bfloat16"), "I4": ("sbuf", [128, 128], "bfloat16"),
+    "BO": ("sbuf", [128, 128], "bfloat16"), "MK": ("sbuf", [128, 16], "float32"),
+    "RB": ("sbuf", [128, 98], "bfloat16"), "RX": ("sbuf", [128, S], "bfloat16"), "K": ("sbuf", [128, S], "float32"),
+    "N0": ("sbuf", [128, 2048], "bfloat16"), "N1": ("sbuf", [128, 2048], "float32"), "ON": ("sbuf", [128, S], "float16"),
+}
+for _i, (_a, _n) in enumerate(CH):
+    SCRATCH["so%d" % _i] = ("dram", [4, 128, _n // 4], "float16")
+    SCRATCH["ly%d" % _i] = ("dram", [4, 128, _n // 4], "float16")
+    SCRATCH["ps%d" % _i] = ("psum", [128, 512], "float32")
+for _i in range(2):
+    SCRATCH["pe%d" % _i] = ("psum", [128, 512], "float32")
+for _s in range(2):
+    for _n, _w, _d in (("SE0", 480, "bfloat16"), ("SE1", 480, "bfloat16"), ("SE2", 480, "bfloat16"), ("SE3", 480, "bfloat16"),
+                       ("TA", S, "float32"), ("TP", S, "float32"), ("FA", S, "bfloat16"), ("FB", S, "bfloat16"),
+                       ("FW", 2064, "bfloat16"), ("UW", 2048, "bfloat16"), ("GW", 2064, "bfloat16"),
+                       ("DG", 3 * S, "bfloat16"), ("DB", S, "float32"), ("VT", S, "bfloat16"), ("VG", 2 * S, "bfloat16"),
+                       ("UG", 6 * S, "bfloat16"), ("UA", S, "float32")):
+        SCRATCH["%s_%d" % (_n, _s)] = ("sbuf", [128, _w], _d)
+
+SEMAPHORES = (["cv", "cs", "ct", "cg", "rl", "se", "sl", "gx", "gl", "gy", "EE", "XX"]
+              + ["ae%d" % r for r in range(4)] + ["ax%d" % r for r in range(4)] + ["al%d" % r for r in range(4)]
+              + ["o%d" % i for i in range(4)] + ["w%d" % i for i in range(4)] + ["ay%d" % i for i in range(4)])
+
+
+def masks(src, cores, topo):
+    others = [c for c in cores if c != src]
+    eng = dict((c, list(topo.engines(src, c))) for c in others)
+    few = min(len(eng[c]) for c in others)
+    far = [c for c in others if len(eng[c]) == few]
+    share = len(eng[far[0]]) // len(far)
+    share = 1 << (share.bit_length() - 1)
+    out = {}
+    for i, c in enumerate(far):
+        out[c] = eng[c][i * share:(i + 1) * share]
+    for c in others:
+        if c not in out:
+            out[c] = [e for e in eng[c] if e not in eng[far[0]]][:4]
+    return out
+
+
+def rank_program(g, core, T, topo):
+    me = T.rank_of(core)
+    if me is None:
+        return
+    add, sub, mult, amin = AluOpType.add, AluOpType.subtract, AluOpType.mult, AluOpType.min
+    act = ActivationFunctionType
+    cores = list(T.cores)
+    N = len(cores)
+    others = [r for r in range(N) if r != me]
+    near = [r for r in others if cores[r] in topo.cores_of(core)]
+    order = near + [r for r in others if r not in near]
+    eng = masks(core, cores, topo)
+    inc = dict((r, len(masks(cores[r], cores, topo)[core])) for r in others)
+
+    queue = {"v": g.vector, "s": g.scalar, "t": g.tensor, "g": g, "y": g.sync}
+    total, waited, hist = {}, {}, {}
+    know = dict((k, {}) for k in queue)
+
+    def wait(k, toks):
+        best = {}
+        for sem, val, clock in toks:
+            if know[k].get(sem, 0) < val and (sem not in best or best[sem][1] < val):
+                best[sem] = (sem, val, clock)
+        todo = [t for t in best.values() if not any(u[0] != t[0] and u[2].get(t[0], 0) >= t[1] for u in best.values())]
+        for sem, val, clock in todo:
+            queue[k].wait_ge(T.sem[sem], val)
+            waited[sem] = max(waited.get(sem, 0), val)
+            for s, v in list(clock.items()) + [(sem, val)]:
+                know[k][s] = max(know[k].get(s, 0), v)
+
+    def hazards(k, rd, wr):
+        toks = []
+        for kind, regs in ((0, rd), (1, wr)):
+            for b, lo, hi, p0, p1 in regs:
+                for lo2, hi2, q0, q1, w2, tok, k2 in hist.get(b, []):
+                    if lo < hi2 and lo2 < hi and p0 < q1 and q0 < p1 and (kind or w2):
+                        if k == "t" and k2 == "t" and kind and b[0] == "p":
+                            continue
+                        toks.append(tok)
+        return toks
+
+    def note(k, rd, wr, tok):
+        for w, regs in ((0, rd), (1, wr)):
+            for b, lo, hi, p0, p1 in regs:
+                hist.setdefault(b, []).append((lo, hi, p0, p1, w, tok, k))
+
+    def reg(b, lo, hi, p0=0, p1=128):
+        return (b, lo, hi, p0, p1)
+
+    def op(k, rd, wr, call):
+        wait(k, hazards(k, rd, wr))
+        sem = "c" + k
+        total[sem] = total.get(sem, 0) + 1
+        clock = dict(know[k])
+        clock[sem] = total[sem]
+        note(k, rd, wr, (sem, total[sem], clock))
+        call().then_inc(T.sem[sem], 1)
+
+    def dma(k, out, in_, sem, full, rd, wr):
+        wait(k, hazards(k, rd, wr))
+        total[sem] = total.get(sem, 0) + 16
+        note(k, rd, wr, (sem, full, dict(know[k]) if full == 16 else {}))
+        queue[k].dma_start(out, in_).then_inc(T.sem[sem], 16)
+
+    def send(src, dst, sems, rd):
+        wait("g", hazards("g", rd, []))
+        trs = []
+        for r in order:
+            rid, pid = topo.addr(cores[r], core)
+            m = 0
+            for e in eng[cores[r]]:
+                m |= 1 << e
+            trs.append(RemoteDMATransfer(dst_ids=[DstId(rid=rid, pnc=pid)], dma_engine_mask=m, remote_sem=T.sem[sems],
+                                         src=T[src][r], dst=T[dst][me]))
+            total["rl"] = total.get("rl", 0) + len(eng[cores[r]])
+        g.remote_dma_fused(trs, local_sem=T.sem["rl"])
+
+    def arrives(sem, buf, srcs):
+        n = sum(inc[r] for r in srcs)
+        total[sem] = total.get(sem, 0) + n
+        for r in srcs:
+            note("r", [], [reg(buf, r, r + 1)], (sem, n, {}))
+
+    def ap(x):
+        b, lo, hi = x
+        return T[b][:, lo:hi]
+
+    def ind(win, wn, lst, c0, n):
+        return T[win][:, 0:wn].indirect(T[lst][:, c0:c0 + n // 16])
+
+    def r3(x):
+        return reg(x[0], x[1], x[2])
+
+    def indreg(win, wn, lst, c0, n):
+        return [reg(win, 0, wn), reg(lst, c0, c0 + n // 16)]
+
+    def pick(k, out, win, wn, lst, c0):
+        n = out[2] - out[1]
+        rd = indreg(win, wn, lst, c0, n)
+        if k == "v":
+            op("v", rd, [r3(out)], lambda: g.vector.tensor_copy(out=ap(out), in_=ind(win, wn, lst, c0, n)))
+        else:
+            op("s", rd, [r3(out)], lambda: g.scalar.activation(out=ap(out), in_=ind(win, wn, lst, c0, n), func=act.Copy))
+
+    def pickop(out, win, wn, lst, c0, other, o):
+        n = out[2] - out[1]
+        op("v", indreg(win, wn, lst, c0, n) + [r3(other)], [r3(out)],
+           lambda: g.vector.tensor_tensor(out=ap(out), in0=ind(win, wn, lst, c0, n), in1=ap(other), op=o))
+
+    def tt(out, a, b, o):
+        op("v", [r3(a), r3(b)], [r3(out)], lambda: g.vector.tensor_tensor(out=ap(out), in0=ap(a), in1=ap(b), op=o))
+
+    def ts(out, a, s1, o1, s2=None, o2=None, more=()):
+        if o2 is None:
+            f = lambda: g.vector.tensor_scalar(out=ap(out), in0=ap(a), scalar1=s1, scalar2=None, op0=o1)
+        else:
+            f = lambda: g.vector.tensor_scalar(out=ap(out), in0=ap(a), scalar1=s1, scalar2=s2, op0=o1, op1=o2)
+        op("v", [r3(a)] + list(more), [r3(out)], f)
+
+    def actv(out, a, func, bias=0.0, scale=1.0, more=()):
+        if func == act.Copy:
+            f = lambda: g.scalar.activation(out=ap(out), in_=ap(a), func=func)
+        else:
+            f = lambda: g.scalar.activation(out=ap(out), in_=ap(a), func=func, bias=bias, scale=scale)
+        op("s", [r3(a)] + list(more), [r3(out)], f)
+
+    def copy(k, out, a):
+        if k == "v":
+            op("v", [r3(a)], [r3(out)], lambda: g.vector.tensor_copy(out=ap(out), in_=ap(a)))
+        else:
+            actv(out, a, act.Copy)
+
+    def mm(out, lhs, rhs, start, stop):
+        op("t", [r3(lhs), r3(rhs)], [r3(out)],
+           lambda: g.tensor.matmul(out=ap(out), lhsT=ap(lhs), rhs=ap(rhs), start=start, stop=stop))
+
+    EYE = ("W", 0, 128)
+    NEG = ("NI", 0, 128)
+
+    dma("g", T.sx[:], T.x[:], "gx", 16, [], [reg("sx", 0, 4)])
+    dma("y", T.se[:, 0::4, :], T.reac[:, 0:98], "se", 96, [], [reg("se", 0, 4, 0, 1)])
+    dma("s", T.se[:, 3::4, 0:30], T.spsend[:], "se", 96, [], [reg("se", 0, 4, 3, 4)])
+    dma("y", T.se[:, 1::4, :], T.reac[:, 98:196], "se", 96, [], [reg("se", 0, 4, 1, 2)])
+    dma("s", T.se[:, 3::4, 30:60], T.rxsend[:], "se", 96, [], [reg("se", 0, 4, 4, 5)])
+    dma("y", T.se[:, 2::4, :], T.rate[:], "se", 96, [], [reg("se", 0, 4, 2, 3)])
+    dma("s", T.se[:, 3::4, 60:98], T.reac[:, 0:38], "se", 96, [], [reg("se", 0, 4, 5, 6)])
+    for j in range(2):
+        dma("s", T.sl[:, j::4, :], T.cons[:, 147 * j:147 * j + 147], "sl", 64, [], [reg("sl", 0, 4, j, j + 1)])
+        dma("y", T.sl[:, 2 + j::4, :], T.prod[:, 147 * j:147 * j + 147], "sl", 64, [], [reg("sl", 0, 4, 2 + j, 3 + j)])
+
+    op("g", [], [reg("IW", 0, 256)], lambda: g.iota(T.IW[:], [[-1, 256]], 256, 1))
+    op("g", [], [reg("IM", 0, 16)], lambda: g.iota(T.IM[:], [[-1, 16]], 128, 1))
+    op("g", [], [reg("IB", 0, 128)], lambda: g.iota(T.IB[:], [[-16, 8], [0, 16]], 128, 1))
+    send("se", "le", "ae%d" % me, [reg("se", 0, 4)])
+    send("sx", "lx", "ax%d" % me, [reg("sx", 0, 4)])
+    send("sl", "ll", "al%d" % me, [reg("sl", 0, 4)])
+    for r in others:
+        arrives("ae%d" % r, "le", [r])
+        arrives("ax%d" % r, "lx", [r])
+        arrives("al%d" % r, "ll", [r])
+
+    for b in ("FW_0", "GW_0", "FW_1", "GW_1"):
+        op("v", [], [reg(b, 2048, 2064)], lambda b=b: g.vector.memset(T[b][:, 2048:2064], 0.0))
+    eq = AluOpType.is_equal
+    ts(("JW", 0, 256), ("IW", 0, 256), 127, AluOpType.bitwise_and)
+    ts(("JM", 0, 16), ("IM", 0, 16), 15, AluOpType.bitwise_and)
+    ts(("JB", 0, 128), ("IB", 0, 128), 4, AluOpType.arith_shift_right)
+    ts(("W", 0, 256), ("JW", 0, 256), 0, eq)
+    ts(("NI", 0, 128), ("JW", 0, 128), 0, eq, -1, mult)
+    ts(("I4", 0, 128), ("JW", 0, 128), 0, eq, 4, mult)
+    ts(("MK", 0, 16), ("JM", 0, 16), 0, eq, 1.0 / 1024, mult)
+    ts(("BO", 0, 128), ("JB", 0, 128), 8, eq)
+
+    for r in [me] + order:
+        b = "se" if r == me else "le"
+        dma("y", T.E32[32 * r:32 * r + 32, :], T[b][r], "EE", 64, [reg(b, r, r + 1)], [reg("E32", 0, 392, 32 * r, 32 * r + 32)])
+    copy("v", ("RB", 0, 98), ("E32", 196, 294))
+    copy("v", ("LST", 0, 354), ("E32", 0, 354))
+    for c in range(16):
+        o, m = ("RX", 98 * c, 98 * c + 98), reg("MK", c, c + 1)
+        if c % 2:
+            actv(o, ("RB", 0, 98), act.Identity, 0.0, T.MK[:, c:c + 1], [m])
+        else:
+            ts(o, ("RB", 0, 98), T.MK[:, c:c + 1], mult, None, None, [m])
+    for i, (a, n) in enumerate(CH):
+        mm(("ps%d" % i, 0, n), ("BO", 0, 128), ("RX", a, a + n), True, True)
+        copy("sv"[i % 2], ("K", a, a + n), ("ps%d" % i, 0, n))
+    last = order[-1]
+    for r in [me] + order:
+        b = "sx" if r == me else "lx"
+        dma("s" if r == last else "y", T.N0[32 * r:32 * r + 32, 0:S], T[b][r], "XX", 64, [reg(b, r, r + 1)],
+            [reg("N0", 0, S, 32 * r, 32 * r + 32)])
+    for r in [me] + order:
+        b = "sl" if r == me else "ll"
+        dma("g", T.CPL[32 * r:32 * r + 32, :], T[b][r], "gl", 64, [reg(b, r, r + 1)], [reg("CPL", 0, 588, 32 * r, 32 * r + 32)])
+
+    RE, SP, RXL = 0, 294, 324
+
+    def border(s, e, win, c0):
+        se = "SE%d_%d" % (e, s)
+        pick("v", (se, 256, 480), win, S, "LST", c0 + 16)
+        pick("s", (se, 0, 256), win, S, "LST", c0)
+
+        def rot(m):
+            return ("W", 32 * (1 + m), 32 * (1 + m) + 128)
+        mm(("pe0", 160, 256), rot(1), (se, 160, 256), True, True)
+        mm(("pe0", 0, 160), rot(0), (se, 320, 480), True, True)
+        mm(("pe1", 64, 224), rot(2), (se, 0, 160), True, True)
+        mm(("pe1", 0, 64), rot(1), (se, 256, 320), True, True)
+        copy("v", (win, S, S + 256), ("pe0", 0, 256))
+        copy("s", (win, S + 256, 2048), ("pe1", 0, 224))
+
+    for s in range(2):
+        def nm(b):
+            return "%s_%d" % (b, s)
+        NW, FW, UW, GW = "N%d" % s, nm("FW"), nm("UW"), nm("GW")
+        border(s, 0, NW, SP)
+
+        def ka(i):
+            a, n = CH[i]
+            pickop((nm("TA"), a, a + n), NW, 2048, "LST", RE + a // 16, ("K", a, a + n), mult)
+
+        def kb(i):
+            a, n = CH[i]
+            pickop((nm("TP"), a, a + n), NW, 2048, "LST", RE + 98 + a // 16, (nm("TA"), a, a + n), mult)
+
+        def whole(i, k):
+            a, n = CH[i]
+            p, fa, fb, f = [(b, a, a + n) for b in (nm("TP"), nm("FA"), nm("FB"), FW)]
+            if k == "s":
+                actv(fa, p, act.Identity, HALF, 1.0)
+                actv(fb, fa, act.Relu, 132.0, -1.0)
+                actv(f, fb, act.Identity, 3.0, -1.0)
+            else:
+                ts(fa, p, 3.4, amin, HALF, add)
+                ts(f, fa, -129.0, add)
+        ka(0)
+        ka(1)
+        kb(0)
+        whole(0, "s")
+        ka(2)
+        kb(1)
+        whole(1, "s")
+        ka(3)
+        kb(2)
+        whole(2, "s")
+        kb(3)
+        whole(3, "v")
+        border(s, 1, FW, RXL)
+        DB, DG = nm("DB"), nm("DG")
+
+        def dv(i, c, first):
+            a, n = CH[i]
+            x = (DB, a, a + n)
+            pickop(x, FW, 2049, "CPL", 98 * c + a // 16, (NW, a, a + n) if first else x, sub if first else add)
+
+        def dsc(i, c, start, stop):
+            a, n = CH[i]
+            x = (DG, S * c + a, S * c + a + n)
+            pick("s", x, FW, 2049, "CPL", 98 * c + a // 16)
+            mm(("ps%d" % i, 0, n), NEG, x, start, stop)
+
+        def keep(i):
+            a, n = CH[i]
+            tt((UW, a, a + n), (DB, a, a + n), ("ps%d" % i, 0, n), AluOpType.is_le)
+        for i in range(3):
+            dsc(i, 1, True, False)
+            dsc(i, 2, False, True)
+        dsc(3, 2, True, True)
+        dv(0, 0, True)
+        dv(1, 0, True)
+        dv(2, 0, True)
+        keep(0)
+        dv(3, 0, True)
+        keep(1)
+        dv(3, 1, False)
+        keep(2)
+        keep(3)
+        border(s, 2, UW, SP)
+        VT, VG = nm("VT"), nm("VG")
+        for i in (2, 3):
+            a, n = VS[i]
+            mm(("ps%d" % i, 0, n), EYE, (FW, a, a + n), True, False)
+        for h in range(2):
+            for i in (0, 1):
+                a, n = VS[i]
+                o = (VT, a, a + n) if h == 0 else (GW, a, a + n)
+                pickop(o, UW, 2048, "LST", RE + 98 * h + a // 16, (FW, a, a + n) if h == 0 else (VT, a, a + n), mult)
+        for i in (2, 3):
+            a, n = VS[i]
+            for h in range(2):
+                x = (VG, S * h + a, S * h + a + n)
+                pick("s", x, UW, 2048, "LST", RE + 98 * h + a // 16)
+                mm(("ps%d" % i, 0, n), ("I4", 0, 128), x, False, h == 1)
+        for i in (2, 3):
+            a, n = VS[i]
+            actv((GW, a, a + n), ("ps%d" % i, 0, n), act.Relu, -8.0, 1.0)
+        border(s, 3, GW, RXL)
+        UA, UG = nm("UA"), nm("UG")
+
+        def uv(i, j):
+            a, n = CH[i]
+            x = (UA, a, a + n)
+            pickop(x, GW, 2049, "CPL", 98 * (3 + j) + a // 16, (NW, a, a + n) if j == 0 else x, add)
+
+        def us(i, j, start, stop):
+            a, n = CH[i]
+            x = (UG, S * j + a, S * j + a + n)
+            pick("s", x, GW, 2049, "CPL", 98 * j + a // 16)
+            mm(("ps%d" % i, 0, n), NEG if j < 3 else EYE, x, start, stop)
+
+        def fin(i):
+            a, n = CH[i]
+            o = ("N1", a, a + n) if s == 0 else ("ON", a, a + n)
+            tt(o, (UA, a, a + n), ("ps%d" % i, 0, n), add)
+            if s == 1:
+                dma("y", T["so%d" % i][:], T.ON[:, a:a + n], "o%d" % i, 16, [r3(o)], [reg("so%d" % i, 0, 4)])
+                dma("y", T["ly%d" % i][me], T.ON[32 * me:32 * me + 32, a:a + n], "w%d" % i, 16,
+                    [reg("ON", a, a + n, 32 * me, 32 * me + 32)], [reg("ly%d" % i, me, me + 1)])
+        for i in range(4):
+            us(i, 0, True, False)
+            us(i, 1, False, False)
+            us(i, 2, False, i != 1)
+            if i == 1:
+                us(i, 5, False, True)
+        uv(0, 0)
+        uv(1, 0)
+        uv(0, 1)
+        uv(1, 1)
+        uv(0, 2)
+        uv(2, 0)
+        fin(0)
+        uv(3, 0)
+        uv(2, 1)
+        fin(1)
+        uv(3, 1)
+        uv(2, 2)
+        uv(3, 2)
+        fin(2)
+        fin(3)
+
+    for i in range(4):
+        arrives("ay%d" % i, "ly%d" % i, others)
+
+    def give(i):
+        send("so%d" % i, "ly%d" % i, "ay%d" % i, [reg("so%d" % i, 0, 4)])
+
+    def store(i):
+        a, n = CH[i]
+        dma("g", T.y[:, a:a + n], T["ly%d" % i][:], "gy", 64, [reg("ly%d" % i, 0, 4)], [])
+    give(0)
+    give(1)
+    give(2)
+    store(0)
+    give(3)
+    store(1)
+    store(2)
+    store(3)
+    for sem in total:
+        if waited.get(sem, 0) < total[sem]:
+            g.wait_ge(T.sem[sem], total[sem])

@@ -2,9 +2,10 @@ from concourse.bass import DstId, RemoteDMATransfer
 from concourse.mybir import AluOpType, ActivationFunctionType
 
 S = 1568
-CH = [(0, 416), (416, 384), (800, 384), (1184, 384)]
-VS = [(0, 448), (448, 448), (896, 416), (1312, 256)]
+AC = [(0, 480), (480, 576), (1056, 512)]
+CO = [(0, 992), (992, 576)]
 HALF = 128.500244140625
+LW = CO[1][1] // 4
 
 SCRATCH = {
     "sx": ("dram", [4, 128, 392], "bfloat16"), "lx": ("dram", [4, 128, 392], "bfloat16"),
@@ -14,27 +15,26 @@ SCRATCH = {
     "IW": ("sbuf", [128, 256], "int32"), "IM": ("sbuf", [128, 16], "int32"), "IB": ("sbuf", [128, 128], "int32"),
     "JW": ("sbuf", [128, 256], "int32"), "JM": ("sbuf", [128, 16], "int32"), "JB": ("sbuf", [128, 128], "int32"),
     "W": ("sbuf", [128, 256], "bfloat16"), "NI": ("sbuf", [128, 128], "bfloat16"), "I4": ("sbuf", [128, 128], "bfloat16"),
-    "BO": ("sbuf", [128, 128], "bfloat16"), "MK": ("sbuf", [128, 16], "float32"),
-    "RB": ("sbuf", [128, 98], "bfloat16"), "RX": ("sbuf", [128, S], "bfloat16"), "K": ("sbuf", [128, S], "float32"),
+    "BO": ("sbuf", [128, 128], "bfloat16"), "MK": ("sbuf", [128, 16], "float32"), "BK": ("sbuf", [128, 2048], "bfloat16"),
+    "RB": ("sbuf", [128, 98], "bfloat16"), "K": ("sbuf", [128, S], "float32"),
     "N0": ("sbuf", [128, 2048], "bfloat16"), "N1": ("sbuf", [128, 2048], "float32"), "ON": ("sbuf", [128, S], "float16"),
+    "LY": ("sbuf", [128, 3 * LW], "float16"), "LF": ("sbuf", [128, 3 * LW], "float32"),
+    "pa": ("psum", [128, 1024], "float32"), "pb": ("psum", [128, 1024], "float32"), "pk": ("psum", [128, 512], "float32"),
+    "pe0": ("psum", [128, 512], "float32"), "pe1": ("psum", [128, 512], "float32"), "pe2": ("psum", [128, 512], "float32"),
+    "so0": ("dram", [4, 128, CO[0][1] // 4], "float16"), "ly0": ("dram", [4, 128, CO[0][1] // 4], "float16"),
+    "so1": ("dram", [4, 128, LW], "float16"),
 }
-for _i, (_a, _n) in enumerate(CH):
-    SCRATCH["so%d" % _i] = ("dram", [4, 128, _n // 4], "float16")
-    SCRATCH["ly%d" % _i] = ("dram", [4, 128, _n // 4], "float16")
-    SCRATCH["ps%d" % _i] = ("psum", [128, 512], "float32")
-for _i in range(2):
-    SCRATCH["pe%d" % _i] = ("psum", [128, 512], "float32")
 for _s in range(2):
     for _n, _w, _d in (("SE0", 480, "bfloat16"), ("SE1", 480, "bfloat16"), ("SE2", 480, "bfloat16"), ("SE3", 480, "bfloat16"),
+                       ("X1", 480, "bfloat16"), ("X2", 480, "bfloat16"),
                        ("TA", S, "float32"), ("TP", S, "float32"), ("FA", S, "bfloat16"), ("FB", S, "bfloat16"),
                        ("FW", 2064, "bfloat16"), ("UW", 2048, "bfloat16"), ("GW", 2064, "bfloat16"),
                        ("DG", 3 * S, "bfloat16"), ("DB", S, "float32"), ("VT", S, "bfloat16"), ("VG", 2 * S, "bfloat16"),
                        ("UG", 6 * S, "bfloat16"), ("UA", S, "float32")):
         SCRATCH["%s_%d" % (_n, _s)] = ("sbuf", [128, _w], _d)
 
-SEMAPHORES = (["cv", "cs", "ct", "cg", "rl", "se", "sl", "gx", "gl", "gy", "EE", "XX"]
-              + ["ae%d" % r for r in range(4)] + ["ax%d" % r for r in range(4)] + ["al%d" % r for r in range(4)]
-              + ["o%d" % i for i in range(4)] + ["w%d" % i for i in range(4)] + ["ay%d" % i for i in range(4)])
+SEMAPHORES = (["cv", "cs", "ct", "cg", "rl", "se", "sl", "gx", "gl", "gy", "yy", "EE", "XX", "o0", "o1", "ay0", "ay1"]
+              + ["%s%d" % (a, r) for a in ("ae", "ax", "al") for r in range(4)])
 
 
 def masks(src, cores, topo):
@@ -49,7 +49,7 @@ def masks(src, cores, topo):
         out[c] = eng[c][i * share:(i + 1) * share]
     for c in others:
         if c not in out:
-            out[c] = [e for e in eng[c] if e not in eng[far[0]]][:4]
+            out[c] = [e for e in eng[c] if e not in eng[far[0]]][0:4:2]
     return out
 
 
@@ -58,6 +58,7 @@ def rank_program(g, core, T, topo):
     if me is None:
         return
     add, sub, mult, amin = AluOpType.add, AluOpType.subtract, AluOpType.mult, AluOpType.min
+    eq, le = AluOpType.is_equal, AluOpType.is_le
     act = ActivationFunctionType
     cores = list(T.cores)
     N = len(cores)
@@ -87,10 +88,15 @@ def rank_program(g, core, T, topo):
         toks = []
         for kind, regs in ((0, rd), (1, wr)):
             for b, lo, hi, p0, p1 in regs:
+                bank = b[0] == "p"
                 for lo2, hi2, q0, q1, w2, tok, k2 in hist.get(b, []):
-                    if lo < hi2 and lo2 < hi and p0 < q1 and q0 < p1 and (kind or w2):
-                        if k == "t" and k2 == "t" and kind and b[0] == "p":
-                            continue
+                    if bank and k2 != k:
+                        hit = lo // 512 <= (hi2 - 1) // 512 and lo2 // 512 <= (hi - 1) // 512
+                    elif bank:
+                        hit = False
+                    else:
+                        hit = lo < hi2 and lo2 < hi and p0 < q1 and q0 < p1 and (kind or w2)
+                    if hit:
                         toks.append(tok)
         return toks
 
@@ -126,161 +132,145 @@ def rank_program(g, core, T, topo):
             for e in eng[cores[r]]:
                 m |= 1 << e
             trs.append(RemoteDMATransfer(dst_ids=[DstId(rid=rid, pnc=pid)], dma_engine_mask=m, remote_sem=T.sem[sems],
-                                         src=T[src][r], dst=T[dst][me]))
+                                         src=T[src][r], dst=dst(r)))
             total["rl"] = total.get("rl", 0) + len(eng[cores[r]])
         g.remote_dma_fused(trs, local_sem=T.sem["rl"])
 
-    def arrives(sem, buf, srcs):
+    def arrives(sem, regs, srcs):
         n = sum(inc[r] for r in srcs)
         total[sem] = total.get(sem, 0) + n
-        for r in srcs:
-            note("r", [], [reg(buf, r, r + 1)], (sem, n, {}))
+        note("r", [], regs, (sem, n, {}))
 
     def ap(x):
-        b, lo, hi = x
-        return T[b][:, lo:hi]
+        return T[x[0]][:, x[1]:x[2]]
 
     def ind(win, wn, lst, c0, n):
         return T[win][:, 0:wn].indirect(T[lst][:, c0:c0 + n // 16])
 
-    def r3(x):
-        return reg(x[0], x[1], x[2])
-
-    def indreg(win, wn, lst, c0, n):
-        return [reg(win, 0, wn), reg(lst, c0, c0 + n // 16)]
-
     def pick(k, out, win, wn, lst, c0):
         n = out[2] - out[1]
-        rd = indreg(win, wn, lst, c0, n)
+        rd = [reg(win, 0, wn), reg(lst, c0, c0 + n // 16)]
         if k == "v":
-            op("v", rd, [r3(out)], lambda: g.vector.tensor_copy(out=ap(out), in_=ind(win, wn, lst, c0, n)))
+            op("v", rd, [reg(*out)], lambda: g.vector.tensor_copy(out=ap(out), in_=ind(win, wn, lst, c0, n)))
         else:
-            op("s", rd, [r3(out)], lambda: g.scalar.activation(out=ap(out), in_=ind(win, wn, lst, c0, n), func=act.Copy))
+            op("s", rd, [reg(*out)], lambda: g.scalar.activation(out=ap(out), in_=ind(win, wn, lst, c0, n), func=act.Copy))
 
     def pickop(out, win, wn, lst, c0, other, o):
         n = out[2] - out[1]
-        op("v", indreg(win, wn, lst, c0, n) + [r3(other)], [r3(out)],
+        op("v", [reg(win, 0, wn), reg(lst, c0, c0 + n // 16), reg(*other)], [reg(*out)],
            lambda: g.vector.tensor_tensor(out=ap(out), in0=ind(win, wn, lst, c0, n), in1=ap(other), op=o))
 
     def tt(out, a, b, o):
-        op("v", [r3(a), r3(b)], [r3(out)], lambda: g.vector.tensor_tensor(out=ap(out), in0=ap(a), in1=ap(b), op=o))
+        op("v", [reg(*a), reg(*b)], [reg(*out)], lambda: g.vector.tensor_tensor(out=ap(out), in0=ap(a), in1=ap(b), op=o))
 
     def ts(out, a, s1, o1, s2=None, o2=None, more=()):
         if o2 is None:
             f = lambda: g.vector.tensor_scalar(out=ap(out), in0=ap(a), scalar1=s1, scalar2=None, op0=o1)
         else:
             f = lambda: g.vector.tensor_scalar(out=ap(out), in0=ap(a), scalar1=s1, scalar2=s2, op0=o1, op1=o2)
-        op("v", [r3(a)] + list(more), [r3(out)], f)
+        op("v", [reg(*a)] + list(more), [reg(*out)], f)
 
     def actv(out, a, func, bias=0.0, scale=1.0, more=()):
         if func == act.Copy:
             f = lambda: g.scalar.activation(out=ap(out), in_=ap(a), func=func)
         else:
             f = lambda: g.scalar.activation(out=ap(out), in_=ap(a), func=func, bias=bias, scale=scale)
-        op("s", [r3(a)] + list(more), [r3(out)], f)
+        op("s", [reg(*a)] + list(more), [reg(*out)], f)
 
     def copy(k, out, a):
         if k == "v":
-            op("v", [r3(a)], [r3(out)], lambda: g.vector.tensor_copy(out=ap(out), in_=ap(a)))
+            op("v", [reg(*a)], [reg(*out)], lambda: g.vector.tensor_copy(out=ap(out), in_=ap(a)))
         else:
             actv(out, a, act.Copy)
 
     def mm(out, lhs, rhs, start, stop):
-        op("t", [r3(lhs), r3(rhs)], [r3(out)],
+        op("t", [reg(*lhs), reg(*rhs)], [reg(*out)],
            lambda: g.tensor.matmul(out=ap(out), lhsT=ap(lhs), rhs=ap(rhs), start=start, stop=stop))
 
-    EYE = ("W", 0, 128)
-    NEG = ("NI", 0, 128)
+    def mmw(pb, p0, lhs, rb, r0, n, start, stop):
+        for c in range(0, n, 512):
+            m = min(512, n - c)
+            mm((pb, p0 + c, p0 + c + m), lhs, (rb, r0 + c, r0 + c + m), start, stop)
+
+    EYE, NEG, I4 = ("W", 0, 128), ("NI", 0, 128), ("I4", 0, 128)
 
     dma("g", T.sx[:], T.x[:], "gx", 16, [], [reg("sx", 0, 4)])
-    dma("y", T.se[:, 0::4, :], T.reac[:, 0:98], "se", 96, [], [reg("se", 0, 4, 0, 1)])
-    dma("s", T.se[:, 3::4, 0:30], T.spsend[:], "se", 96, [], [reg("se", 0, 4, 3, 4)])
-    dma("y", T.se[:, 1::4, :], T.reac[:, 98:196], "se", 96, [], [reg("se", 0, 4, 1, 2)])
-    dma("s", T.se[:, 3::4, 30:60], T.rxsend[:], "se", 96, [], [reg("se", 0, 4, 4, 5)])
-    dma("y", T.se[:, 2::4, :], T.rate[:], "se", 96, [], [reg("se", 0, 4, 2, 3)])
-    dma("s", T.se[:, 3::4, 60:98], T.reac[:, 0:38], "se", 96, [], [reg("se", 0, 4, 5, 6)])
+    for k, j, a, b, t in (("y", 0, 0, 98, T.reac[:, 0:98]), ("s", 3, 0, 30, T.spsend[:]), ("y", 1, 0, 98, T.reac[:, 98:196]),
+                          ("s", 3, 30, 60, T.rxsend[:]), ("y", 2, 0, 98, T.rate[:]),
+                          ("s", 3, 60, 98, T.reac[:, 0:38])):
+        dma(k, T.se[:, j::4, a:b], t, "se", 96, [], [reg("se", 0, 4, 30 * j + a // 30, 30 * j + a // 30 + 1)])
     for j in range(2):
         dma("s", T.sl[:, j::4, :], T.cons[:, 147 * j:147 * j + 147], "sl", 64, [], [reg("sl", 0, 4, j, j + 1)])
         dma("y", T.sl[:, 2 + j::4, :], T.prod[:, 147 * j:147 * j + 147], "sl", 64, [], [reg("sl", 0, 4, 2 + j, 3 + j)])
 
-    op("g", [], [reg("IW", 0, 256)], lambda: g.iota(T.IW[:], [[-1, 256]], 256, 1))
-    op("g", [], [reg("IM", 0, 16)], lambda: g.iota(T.IM[:], [[-1, 16]], 128, 1))
     op("g", [], [reg("IB", 0, 128)], lambda: g.iota(T.IB[:], [[-16, 8], [0, 16]], 128, 1))
-    send("se", "le", "ae%d" % me, [reg("se", 0, 4)])
-    send("sx", "lx", "ax%d" % me, [reg("sx", 0, 4)])
-    send("sl", "ll", "al%d" % me, [reg("sl", 0, 4)])
-    for r in others:
-        arrives("ae%d" % r, "le", [r])
-        arrives("ax%d" % r, "lx", [r])
-        arrives("al%d" % r, "ll", [r])
+    op("g", [], [reg("IM", 0, 16)], lambda: g.iota(T.IM[:], [[-1, 16]], 128, 1))
+    op("g", [], [reg("IW", 0, 256)], lambda: g.iota(T.IW[:], [[-1, 256]], 256, 1))
+    for a, b, c in (("se", "le", "ae"), ("sx", "lx", "ax"), ("sl", "ll", "al")):
+        send(a, lambda r: T[b][me], "%s%d" % (c, me), [reg(a, 0, 4)])
+        for r in others:
+            arrives("%s%d" % (c, r), [reg(b, r, r + 1)], [r])
 
     for b in ("FW_0", "GW_0", "FW_1", "GW_1"):
-        op("v", [], [reg(b, 2048, 2064)], lambda b=b: g.vector.memset(T[b][:, 2048:2064], 0.0))
-    eq = AluOpType.is_equal
-    ts(("JW", 0, 256), ("IW", 0, 256), 127, AluOpType.bitwise_and)
-    ts(("JM", 0, 16), ("IM", 0, 16), 15, AluOpType.bitwise_and)
+        op("v", [], [reg(b, 2048, 2064)], lambda: g.vector.memset(T[b][:, 2048:2064], 0.0))
     ts(("JB", 0, 128), ("IB", 0, 128), 4, AluOpType.arith_shift_right)
+    ts(("JM", 0, 16), ("IM", 0, 16), 15, AluOpType.bitwise_and)
+    ts(("BO", 0, 128), ("JB", 0, 128), 8, eq)
+    ts(("MK", 0, 16), ("JM", 0, 16), 0, eq, 1.0 / 1024, mult)
+    for c in range(16):
+        o, m = ("BK", 128 * c, 128 * c + 128), reg("MK", c, c + 1)
+        if c % 2:
+            actv(o, ("BO", 0, 128), act.Identity, 0.0, T.MK[:, c:c + 1], [m])
+        else:
+            ts(o, ("BO", 0, 128), T.MK[:, c:c + 1], mult, None, None, [m])
+    ts(("JW", 0, 256), ("IW", 0, 256), 127, AluOpType.bitwise_and)
     ts(("W", 0, 256), ("JW", 0, 256), 0, eq)
     ts(("NI", 0, 128), ("JW", 0, 128), 0, eq, -1, mult)
     ts(("I4", 0, 128), ("JW", 0, 128), 0, eq, 4, mult)
-    ts(("MK", 0, 16), ("JM", 0, 16), 0, eq, 1.0 / 1024, mult)
-    ts(("BO", 0, 128), ("JB", 0, 128), 8, eq)
 
+    for sem, a, b, buf, n in (("EE", "se", "le", "E32", 392), ("XX", "sx", "lx", "N0", S)):
+        for r in [me] + order:
+            t = a if r == me else b
+            dma("y", T[buf][32 * r:32 * r + 32, 0:n], T[t][r], sem, 64, [reg(t, r, r + 1)], [reg(buf, 0, n, 32 * r, 32 * r + 32)])
     for r in [me] + order:
-        b = "se" if r == me else "le"
-        dma("y", T.E32[32 * r:32 * r + 32, :], T[b][r], "EE", 64, [reg(b, r, r + 1)], [reg("E32", 0, 392, 32 * r, 32 * r + 32)])
+        t = "sl" if r == me else "ll"
+        dma("g", T.CPL[32 * r:32 * r + 32, :], T[t][r], "gl", 64, [reg(t, r, r + 1)], [reg("CPL", 0, 588, 32 * r, 32 * r + 32)])
     copy("v", ("RB", 0, 98), ("E32", 196, 294))
     copy("v", ("LST", 0, 354), ("E32", 0, 354))
-    for c in range(16):
-        o, m = ("RX", 98 * c, 98 * c + 98), reg("MK", c, c + 1)
-        if c % 2:
-            actv(o, ("RB", 0, 98), act.Identity, 0.0, T.MK[:, c:c + 1], [m])
-        else:
-            ts(o, ("RB", 0, 98), T.MK[:, c:c + 1], mult, None, None, [m])
-    for i, (a, n) in enumerate(CH):
-        mm(("ps%d" % i, 0, n), ("BO", 0, 128), ("RX", a, a + n), True, True)
-        copy("sv"[i % 2], ("K", a, a + n), ("ps%d" % i, 0, n))
-    last = order[-1]
-    for r in [me] + order:
-        b = "sx" if r == me else "lx"
-        dma("s" if r == last else "y", T.N0[32 * r:32 * r + 32, 0:S], T[b][r], "XX", 64, [reg(b, r, r + 1)],
-            [reg("N0", 0, S, 32 * r, 32 * r + 32)])
-    for r in [me] + order:
-        b = "sl" if r == me else "ll"
-        dma("g", T.CPL[32 * r:32 * r + 32, :], T[b][r], "gl", 64, [reg(b, r, r + 1)], [reg("CPL", 0, 588, 32 * r, 32 * r + 32)])
+
+    def spread(p, p0, c0, c1):
+        for c in range(c0, c1):
+            a = p0 + 98 * (c - c0)
+            mm((p, a, a + 98), ("BK", 128 * c, 128 * c + 128), ("RB", 0, 98), True, True)
+    for k, p, p0, c0, c1 in (("s", "pa", 0, 4, 9), ("v", "pa", 512, 9, 13), ("s", "pb", 0, 13, 16)):
+        spread(p, p0, c0, c1)
+        copy(k, ("K", 98 * c0, 98 * c1), (p, p0, p0 + 98 * (c1 - c0)))
 
     RE, SP, RXL = 0, 294, 324
 
     def border(s, e, win, c0):
         se = "SE%d_%d" % (e, s)
-        pick("v", (se, 256, 480), win, S, "LST", c0 + 16)
-        pick("s", (se, 0, 256), win, S, "LST", c0)
-
-        def rot(m):
-            return ("W", 32 * (1 + m), 32 * (1 + m) + 128)
-        mm(("pe0", 160, 256), rot(1), (se, 160, 256), True, True)
-        mm(("pe0", 0, 160), rot(0), (se, 320, 480), True, True)
-        mm(("pe1", 64, 224), rot(2), (se, 0, 160), True, True)
-        mm(("pe1", 0, 64), rot(1), (se, 256, 320), True, True)
-        copy("v", (win, S, S + 256), ("pe0", 0, 256))
-        copy("s", (win, S + 256, 2048), ("pe1", 0, 224))
+        pick("v", (se, 224, 480), win, S, "LST", c0 + 14)
+        pick("s", (se, 0, 224), win, S, "LST", c0)
+        for m, k in ((2, "s"), (0, "v"), (1, "s")):
+            mm(("pe%d" % m, 0, 160), ("W", 32 * (1 + m), 32 * (1 + m) + 128), (se, 160 * (2 - m), 160 * (3 - m)), True, True)
+            copy(k, (win, S + 160 * m, S + 160 * m + 160), ("pe%d" % m, 0, 160))
 
     for s in range(2):
         def nm(b):
             return "%s_%d" % (b, s)
         NW, FW, UW, GW = "N%d" % s, nm("FW"), nm("UW"), nm("GW")
         border(s, 0, NW, SP)
+        if s == 0:
+            spread("pk", 0, 0, 5)
 
-        def ka(i):
-            a, n = CH[i]
-            pickop((nm("TA"), a, a + n), NW, 2048, "LST", RE + a // 16, ("K", a, a + n), mult)
-
-        def kb(i):
-            a, n = CH[i]
-            pickop((nm("TP"), a, a + n), NW, 2048, "LST", RE + 98 + a // 16, (nm("TA"), a, a + n), mult)
+        def kx(i, h):
+            a, n = AC[i]
+            o, x = ((nm("TA"), a, a + n), ("K", a, a + n)) if h == 0 else ((nm("TP"), a, a + n), (nm("TA"), a, a + n))
+            pickop(o, NW, 2048, "LST", RE + 98 * h + a // 16, x, mult)
 
         def whole(i, k):
-            a, n = CH[i]
+            a, n = AC[i]
             p, fa, fb, f = [(b, a, a + n) for b in (nm("TP"), nm("FA"), nm("FB"), FW)]
             if k == "s":
                 actv(fa, p, act.Identity, HALF, 1.0)
@@ -289,128 +279,113 @@ def rank_program(g, core, T, topo):
             else:
                 ts(fa, p, 3.4, amin, HALF, add)
                 ts(f, fa, -129.0, add)
-        ka(0)
-        ka(1)
-        kb(0)
-        whole(0, "s")
-        ka(2)
-        kb(1)
+        n = AC[0][1]
+        pick("s", (nm("X2"), 0, n), NW, 2048, "LST", RE + 98)
+        mm(("pa", 0, n), EYE, (nm("X2"), 0, n), True, True)
+        pick("s", (nm("X1"), 0, n), NW, 2048, "LST", RE)
+        kx(1, 0)
+        kx(1, 1)
         whole(1, "s")
-        ka(3)
-        kb(2)
-        whole(2, "s")
-        kb(3)
-        whole(3, "v")
+        tt((nm("TA"), 0, n), ("pa", 0, n), (nm("X1"), 0, n), mult)
+        tt((nm("TP"), 0, n), ("pk", 0, n), (nm("TA"), 0, n), mult)
+        whole(0, "s")
+        kx(2, 0)
+        kx(2, 1)
+        whole(2, "v")
         border(s, 1, FW, RXL)
         DB, DG = nm("DB"), nm("DG")
-
-        def dv(i, c, first):
-            a, n = CH[i]
-            x = (DB, a, a + n)
-            pickop(x, FW, 2049, "CPL", 98 * c + a // 16, (NW, a, a + n) if first else x, sub if first else add)
-
-        def dsc(i, c, start, stop):
-            a, n = CH[i]
-            x = (DG, S * c + a, S * c + a + n)
-            pick("s", x, FW, 2049, "CPL", 98 * c + a // 16)
-            mm(("ps%d" % i, 0, n), NEG, x, start, stop)
-
-        def keep(i):
-            a, n = CH[i]
-            tt((UW, a, a + n), (DB, a, a + n), ("ps%d" % i, 0, n), AluOpType.is_le)
-        for i in range(3):
-            dsc(i, 1, True, False)
-            dsc(i, 2, False, True)
-        dsc(3, 2, True, True)
-        dv(0, 0, True)
-        dv(1, 0, True)
-        dv(2, 0, True)
-        keep(0)
-        dv(3, 0, True)
-        keep(1)
-        dv(3, 1, False)
-        keep(2)
-        keep(3)
+        A = 896
+        D = [(0, 608, "pa"), (608, A - 608, "pb")]
+        for a, n, p in D:
+            for c in range(3):
+                pick("s", (DG, S * c + a, S * c + a + n), FW, 2049, "CPL", 98 * c + a // 16)
+                mmw(p, 0, EYE, DG, S * c + a, n, c == 0, c == 2)
+        for c in range(3):
+            pickop((DB, A, S), FW, 2049, "CPL", 98 * c + A // 16, (NW if c == 0 else DB, A, S), sub if c == 0 else add)
+        ts((UW, A, S), (DB, A, S), 0.0, le)
+        for a, n, p in D:
+            tt((UW, a, a + n), (p, 0, n), (NW, a, a + n), le)
         border(s, 2, UW, SP)
         VT, VG = nm("VT"), nm("VG")
-        for i in (2, 3):
-            a, n = VS[i]
-            mm(("ps%d" % i, 0, n), EYE, (FW, a, a + n), True, False)
+        A = 960
+        mmw("pb", 0, EYE, FW, A, S - A, True, False)
+        pick("s", (VG, A, S), UW, 2048, "LST", RE + A // 16)
+        mmw("pb", 0, I4, VG, A, S - A, False, False)
+        for a, n in ((A, 512), (A + 512, S - A - 512)):
+            pick("s", (VG, S + a, S + a + n), UW, 2048, "LST", RE + 98 + a // 16)
+            mmw("pb", a - A, I4, VG, S + a, n, False, True)
         for h in range(2):
-            for i in (0, 1):
-                a, n = VS[i]
-                o = (VT, a, a + n) if h == 0 else (GW, a, a + n)
-                pickop(o, UW, 2048, "LST", RE + 98 * h + a // 16, (FW, a, a + n) if h == 0 else (VT, a, a + n), mult)
-        for i in (2, 3):
-            a, n = VS[i]
-            for h in range(2):
-                x = (VG, S * h + a, S * h + a + n)
-                pick("s", x, UW, 2048, "LST", RE + 98 * h + a // 16)
-                mm(("ps%d" % i, 0, n), ("I4", 0, 128), x, False, h == 1)
-        for i in (2, 3):
-            a, n = VS[i]
-            actv((GW, a, a + n), ("ps%d" % i, 0, n), act.Relu, -8.0, 1.0)
+            pickop((VT, 0, A) if h == 0 else (GW, 0, A), UW, 2048, "LST", RE + 98 * h, (FW, 0, A) if h == 0 else (VT, 0, A), mult)
+        for a, n in ((A, 512), (A + 512, S - A - 512)):
+            actv((GW, a, a + n), ("pb", a - A, a - A + n), act.Relu, -8.0, 1.0)
         border(s, 3, GW, RXL)
         UA, UG = nm("UA"), nm("UG")
+        out = "N1" if s == 0 else "ON"
 
-        def uv(i, j):
-            a, n = CH[i]
-            x = (UA, a, a + n)
-            pickop(x, GW, 2049, "CPL", 98 * (3 + j) + a // 16, (NW, a, a + n) if j == 0 else x, add)
+        def uv(a, n, j):
+            acc = (UA, a, a + n)
+            pickop((out, a, a + n) if j == 5 else acc, GW, 2049, "CPL", 98 * j + a // 16,
+                   (NW, a, a + n) if j == 0 else acc, sub if j in (0, 3) else add)
 
-        def us(i, j, start, stop):
-            a, n = CH[i]
-            x = (UG, S * j + a, S * j + a + n)
-            pick("s", x, GW, 2049, "CPL", 98 * j + a // 16)
-            mm(("ps%d" % i, 0, n), NEG if j < 3 else EYE, x, start, stop)
+        def us(a, n, j, p0):
+            pick("s", (UG, S * j + a, S * j + a + n), GW, 2049, "CPL", 98 * j + a // 16)
+            mmw("pa", p0, NEG if j < 3 else EYE, UG, S * j + a, n, j == 0, j == 5)
 
-        def fin(i):
-            a, n = CH[i]
-            o = ("N1", a, a + n) if s == 0 else ("ON", a, a + n)
-            tt(o, (UA, a, a + n), ("ps%d" % i, 0, n), add)
-            if s == 1:
-                dma("y", T["so%d" % i][:], T.ON[:, a:a + n], "o%d" % i, 16, [r3(o)], [reg("so%d" % i, 0, 4)])
-                dma("y", T["ly%d" % i][me], T.ON[32 * me:32 * me + 32, a:a + n], "w%d" % i, 16,
-                    [reg("ON", a, a + n, 32 * me, 32 * me + 32)], [reg("ly%d" % i, me, me + 1)])
-        for i in range(4):
-            us(i, 0, True, False)
-            us(i, 1, False, False)
-            us(i, 2, False, i != 1)
-            if i == 1:
-                us(i, 5, False, True)
-        uv(0, 0)
-        uv(1, 0)
-        uv(0, 1)
-        uv(1, 1)
-        uv(0, 2)
-        uv(2, 0)
-        fin(0)
-        uv(3, 0)
-        uv(2, 1)
-        fin(1)
-        uv(3, 1)
-        uv(2, 2)
-        uv(3, 2)
-        fin(2)
-        fin(3)
+        def fin(a, n, p0):
+            tt((out, a, a + n), ("pa", p0, p0 + n), (NW, a, a + n), add)
 
-    for i in range(4):
-        arrives("ay%d" % i, "ly%d" % i, others)
+        def ship(i):
+            a, n = CO[i]
+            dma("y", T["so%d" % i][:], T.ON[:, a:a + n], "o%d" % i, 16, [reg("ON", a, a + n)], [reg("so%d" % i, 0, 4)])
+        if s == 0:
+            for j in range(5):
+                us(0, 800, j, 0)
+            us(0, 512, 5, 0)
+            us(512, 288, 5, 512)
+            for j in range(6):
+                uv(800, 768, j)
+            fin(0, 512, 0)
+            fin(512, 288, 512)
+        else:
+            for j in range(6):
+                us(0, 512, j, 0)
+            for j in range(6):
+                us(992, 288, j, 512)
+            for j in range(6):
+                uv(512, 480, j)
+            uv(1280, 288, 0)
+            fin(0, 512, 0)
+            ship(0)
+            for j in range(1, 6):
+                uv(1280, 288, j)
+            fin(992, 288, 512)
+            ship(1)
 
-    def give(i):
-        send("so%d" % i, "ly%d" % i, "ay%d" % i, [reg("so%d" % i, 0, 4)])
+    mine = slice(32 * me, 32 * me + 32)
+    parts = [(lo, hi) for lo, hi in ((0, me), (me + 1, N)) if lo < hi]
+    full = 16 * (2 + len(parts))
 
-    def store(i):
-        a, n = CH[i]
-        dma("g", T.y[:, a:a + n], T["ly%d" % i][:], "gy", 64, [reg("ly%d" % i, 0, 4)], [])
-    give(0)
-    give(1)
-    give(2)
-    store(0)
-    give(3)
-    store(1)
-    store(2)
-    store(3)
+    def own(i):
+        a, n = CO[i]
+        dma("g", T.y[mine, a:a + n], T.ON[mine, a:a + n], "gy", full, [reg("ON", a, a + n)], [])
+
+    def slot(r, q):
+        i = [c for c in range(N) if c != r].index(q)
+        return LW * i, LW * i + LW
+    own(0)
+    send("so0", lambda r: T.ly0[me], "ay0", [reg("so0", 0, 4)])
+    arrives("ay0", [reg("ly0", r, r + 1) for r in others], others)
+    own(1)
+    send("so1", lambda r: T.LY[:, slot(r, me)[0]:slot(r, me)[1]], "ay1", [reg("so1", 0, 4)])
+    arrives("ay1", [reg("LY", 0, 3 * LW)], others)
+    a, n = CO[0]
+    for lo, hi in parts:
+        dma("g", T.y[32 * lo:32 * hi, a:a + n], T.ly0[lo:hi], "gy", full, [reg("ly0", lo, hi)], [])
+    copy("v", ("LF", 0, 3 * LW), ("LY", 0, 3 * LW))
+    a, n = CO[1]
+    for i, r in enumerate(others):
+        dma("s" if i == 1 else "y", T.y[32 * r:32 * r + 32, a:a + n], T.LF[:, LW * i:LW * i + LW], "yy", 48,
+            [reg("LF", LW * i, LW * i + LW)], [])
     for sem in total:
         if waited.get(sem, 0) < total[sem]:
             g.wait_ge(T.sem[sem], total[sem])

from concourse.bass import DstId, RemoteDMATransfer
from concourse.mybir import AluOpType, ActivationFunctionType

S = 1568
AC = [(0, 480), (480, 576), (1056, 512)]
CO = [(0, 992), (992, 576)]
HALF = 128.500244140625
LW = CO[1][1] // 4

SCRATCH = {
    "sx": ("dram", [4, 128, 392], "bfloat16"), "lx": ("dram", [4, 128, 392], "bfloat16"),
    "se": ("dram", [4, 128, 98], "int32"), "le": ("dram", [4, 128, 98], "int32"),
    "sl": ("dram", [4, 128, 147], "int32"), "ll": ("dram", [4, 128, 147], "int32"),
    "E32": ("sbuf", [128, 392], "int32"), "LST": ("sbuf", [128, 392], "uint16"), "CPL": ("sbuf", [128, 588], "uint16"),
    "IW": ("sbuf", [128, 256], "int32"), "IM": ("sbuf", [128, 16], "int32"), "IB": ("sbuf", [128, 128], "int32"),
    "JW": ("sbuf", [128, 256], "int32"), "JM": ("sbuf", [128, 16], "int32"), "JB": ("sbuf", [128, 128], "int32"),
    "W": ("sbuf", [128, 256], "bfloat16"), "NI": ("sbuf", [128, 128], "bfloat16"), "I4": ("sbuf", [128, 128], "bfloat16"),
    "BO": ("sbuf", [128, 128], "bfloat16"), "MK": ("sbuf", [128, 16], "float32"), "BK": ("sbuf", [128, 2048], "bfloat16"),
    "RB": ("sbuf", [128, 98], "bfloat16"), "K": ("sbuf", [128, S], "float32"),
    "N0": ("sbuf", [128, 2048], "bfloat16"), "N1": ("sbuf", [128, 2048], "float32"), "ON": ("sbuf", [128, S], "float16"),
    "LY": ("sbuf", [128, 3 * LW], "float16"), "LF": ("sbuf", [128, 3 * LW], "float32"),
    "pa": ("psum", [128, 1024], "float32"), "pb": ("psum", [128, 1024], "float32"), "pk": ("psum", [128, 512], "float32"),
    "pe0": ("psum", [128, 512], "float32"), "pe1": ("psum", [128, 512], "float32"), "pe2": ("psum", [128, 512], "float32"),
    "so0": ("dram", [4, 128, CO[0][1] // 4], "float16"), "ly0": ("dram", [4, 128, CO[0][1] // 4], "float16"),
    "so1": ("dram", [4, 128, LW], "float16"),
}
for _s in range(2):
    for _n, _w, _d in (("SE0", 480, "bfloat16"), ("SE1", 480, "bfloat16"), ("SE2", 480, "bfloat16"), ("SE3", 480, "bfloat16"),
                       ("X1", 480, "bfloat16"), ("X2", 480, "bfloat16"),
                       ("TA", S, "float32"), ("TP", S, "float32"), ("FA", S, "bfloat16"), ("FB", S, "bfloat16"),
                       ("FW", 2064, "bfloat16"), ("UW", 2048, "bfloat16"), ("GW", 2064, "bfloat16"),
                       ("DG", 3 * S, "bfloat16"), ("DB", S, "float32"), ("VT", S, "bfloat16"), ("VG", 2 * S, "bfloat16"),
                       ("UG", 6 * S, "bfloat16"), ("UA", S, "float32")):
        SCRATCH["%s_%d" % (_n, _s)] = ("sbuf", [128, _w], _d)

SEMAPHORES = (["cv", "cs", "ct", "cg", "rl", "se", "sl", "gx", "gl", "gy", "yy", "EE", "XX", "o0", "o1", "ay0", "ay1"]
              + ["%s%d" % (a, r) for a in ("ae", "ax", "al") for r in range(4)])


def masks(src, cores, topo):
    others = [c for c in cores if c != src]
    eng = dict((c, list(topo.engines(src, c))) for c in others)
    few = min(len(eng[c]) for c in others)
    far = [c for c in others if len(eng[c]) == few]
    share = len(eng[far[0]]) // len(far)
    share = 1 << (share.bit_length() - 1)
    out = {}
    for i, c in enumerate(far):
        out[c] = eng[c][i * share:(i + 1) * share]
    for c in others:
        if c not in out:
            out[c] = [e for e in eng[c] if e not in eng[far[0]]][0:4:2]
    return out


def rank_program(g, core, T, topo):
    me = T.rank_of(core)
    if me is None:
        return
    add, sub, mult, amin = AluOpType.add, AluOpType.subtract, AluOpType.mult, AluOpType.min
    eq, le = AluOpType.is_equal, AluOpType.is_le
    act = ActivationFunctionType
    cores = list(T.cores)
    N = len(cores)
    others = [r for r in range(N) if r != me]
    near = [r for r in others if cores[r] in topo.cores_of(core)]
    order = near + [r for r in others if r not in near]
    eng = masks(core, cores, topo)
    inc = dict((r, len(masks(cores[r], cores, topo)[core])) for r in others)

    queue = {"v": g.vector, "s": g.scalar, "t": g.tensor, "g": g, "y": g.sync}
    total, waited, hist = {}, {}, {}
    know = dict((k, {}) for k in queue)

    def wait(k, toks):
        best = {}
        for sem, val, clock in toks:
            if know[k].get(sem, 0) < val and (sem not in best or best[sem][1] < val):
                best[sem] = (sem, val, clock)
        todo = [t for t in best.values() if not any(u[0] != t[0] and u[2].get(t[0], 0) >= t[1] for u in best.values())]
        for sem, val, clock in todo:
            queue[k].wait_ge(T.sem[sem], val)
            waited[sem] = max(waited.get(sem, 0), val)
            for s, v in list(clock.items()) + [(sem, val)]:
                know[k][s] = max(know[k].get(s, 0), v)

    def hazards(k, rd, wr):
        toks = []
        for kind, regs in ((0, rd), (1, wr)):
            for b, lo, hi, p0, p1 in regs:
                bank = b[0] == "p"
                for lo2, hi2, q0, q1, w2, tok, k2 in hist.get(b, []):
                    if bank and k2 != k:
                        hit = lo // 512 <= (hi2 - 1) // 512 and lo2 // 512 <= (hi - 1) // 512
                    elif bank:
                        hit = False
                    else:
                        hit = lo < hi2 and lo2 < hi and p0 < q1 and q0 < p1 and (kind or w2)
                    if hit:
                        toks.append(tok)
        return toks

    def note(k, rd, wr, tok):
        for w, regs in ((0, rd), (1, wr)):
            for b, lo, hi, p0, p1 in regs:
                hist.setdefault(b, []).append((lo, hi, p0, p1, w, tok, k))

    def reg(b, lo, hi, p0=0, p1=128):
        return (b, lo, hi, p0, p1)

    def op(k, rd, wr, call):
        wait(k, hazards(k, rd, wr))
        sem = "c" + k
        total[sem] = total.get(sem, 0) + 1
        clock = dict(know[k])
        clock[sem] = total[sem]
        note(k, rd, wr, (sem, total[sem], clock))
        call().then_inc(T.sem[sem], 1)

    def dma(k, out, in_, sem, full, rd, wr):
        wait(k, hazards(k, rd, wr))
        total[sem] = total.get(sem, 0) + 16
        note(k, rd, wr, (sem, full, dict(know[k]) if full == 16 else {}))
        queue[k].dma_start(out, in_).then_inc(T.sem[sem], 16)

    def send(src, dst, sems, rd):
        wait("g", hazards("g", rd, []))
        trs = []
        for r in order:
            rid, pid = topo.addr(cores[r], core)
            m = 0
            for e in eng[cores[r]]:
                m |= 1 << e
            trs.append(RemoteDMATransfer(dst_ids=[DstId(rid=rid, pnc=pid)], dma_engine_mask=m, remote_sem=T.sem[sems],
                                         src=T[src][r], dst=dst(r)))
            total["rl"] = total.get("rl", 0) + len(eng[cores[r]])
        g.remote_dma_fused(trs, local_sem=T.sem["rl"])

    def arrives(sem, regs, srcs):
        n = sum(inc[r] for r in srcs)
        total[sem] = total.get(sem, 0) + n
        note("r", [], regs, (sem, n, {}))

    def ap(x):
        return T[x[0]][:, x[1]:x[2]]

    def ind(win, wn, lst, c0, n):
        return T[win][:, 0:wn].indirect(T[lst][:, c0:c0 + n // 16])

    def pick(k, out, win, wn, lst, c0):
        n = out[2] - out[1]
        rd = [reg(win, 0, wn), reg(lst, c0, c0 + n // 16)]
        if k == "v":
            op("v", rd, [reg(*out)], lambda: g.vector.tensor_copy(out=ap(out), in_=ind(win, wn, lst, c0, n)))
        else:
            op("s", rd, [reg(*out)], lambda: g.scalar.activation(out=ap(out), in_=ind(win, wn, lst, c0, n), func=act.Copy))

    def pickop(out, win, wn, lst, c0, other, o):
        n = out[2] - out[1]
        op("v", [reg(win, 0, wn), reg(lst, c0, c0 + n // 16), reg(*other)], [reg(*out)],
           lambda: g.vector.tensor_tensor(out=ap(out), in0=ind(win, wn, lst, c0, n), in1=ap(other), op=o))

    def tt(out, a, b, o):
        op("v", [reg(*a), reg(*b)], [reg(*out)], lambda: g.vector.tensor_tensor(out=ap(out), in0=ap(a), in1=ap(b), op=o))

    def ts(out, a, s1, o1, s2=None, o2=None, more=()):
        if o2 is None:
            f = lambda: g.vector.tensor_scalar(out=ap(out), in0=ap(a), scalar1=s1, scalar2=None, op0=o1)
        else:
            f = lambda: g.vector.tensor_scalar(out=ap(out), in0=ap(a), scalar1=s1, scalar2=s2, op0=o1, op1=o2)
        op("v", [reg(*a)] + list(more), [reg(*out)], f)

    def actv(out, a, func, bias=0.0, scale=1.0, more=()):
        if func == act.Copy:
            f = lambda: g.scalar.activation(out=ap(out), in_=ap(a), func=func)
        else:
            f = lambda: g.scalar.activation(out=ap(out), in_=ap(a), func=func, bias=bias, scale=scale)
        op("s", [reg(*a)] + list(more), [reg(*out)], f)

    def copy(k, out, a):
        if k == "v":
            op("v", [reg(*a)], [reg(*out)], lambda: g.vector.tensor_copy(out=ap(out), in_=ap(a)))
        else:
            actv(out, a, act.Copy)

    def mm(out, lhs, rhs, start, stop):
        op("t", [reg(*lhs), reg(*rhs)], [reg(*out)],
           lambda: g.tensor.matmul(out=ap(out), lhsT=ap(lhs), rhs=ap(rhs), start=start, stop=stop))

    def mmw(pb, p0, lhs, rb, r0, n, start, stop):
        for c in range(0, n, 512):
            m = min(512, n - c)
            mm((pb, p0 + c, p0 + c + m), lhs, (rb, r0 + c, r0 + c + m), start, stop)

    EYE, NEG, I4 = ("W", 0, 128), ("NI", 0, 128), ("I4", 0, 128)

    dma("g", T.sx[:], T.x[:], "gx", 16, [], [reg("sx", 0, 4)])
    for k, j, a, b, t in (("y", 0, 0, 98, T.reac[:, 0:98]), ("s", 3, 0, 30, T.spsend[:]), ("y", 1, 0, 98, T.reac[:, 98:196]),
                          ("s", 3, 30, 60, T.rxsend[:]), ("y", 2, 0, 98, T.rate[:]),
                          ("s", 3, 60, 98, T.reac[:, 0:38])):
        dma(k, T.se[:, j::4, a:b], t, "se", 96, [], [reg("se", 0, 4, 30 * j + a // 30, 30 * j + a // 30 + 1)])
    for j in range(2):
        dma("s", T.sl[:, j::4, :], T.cons[:, 147 * j:147 * j + 147], "sl", 64, [], [reg("sl", 0, 4, j, j + 1)])
        dma("y", T.sl[:, 2 + j::4, :], T.prod[:, 147 * j:147 * j + 147], "sl", 64, [], [reg("sl", 0, 4, 2 + j, 3 + j)])

    op("g", [], [reg("IB", 0, 128)], lambda: g.iota(T.IB[:], [[-16, 8], [0, 16]], 128, 1))
    op("g", [], [reg("IM", 0, 16)], lambda: g.iota(T.IM[:], [[-1, 16]], 128, 1))
    op("g", [], [reg("IW", 0, 256)], lambda: g.iota(T.IW[:], [[-1, 256]], 256, 1))
    for a, b, c in (("se", "le", "ae"), ("sx", "lx", "ax"), ("sl", "ll", "al")):
        send(a, lambda r: T[b][me], "%s%d" % (c, me), [reg(a, 0, 4)])
        for r in others:
            arrives("%s%d" % (c, r), [reg(b, r, r + 1)], [r])

    for b in ("FW_0", "GW_0", "FW_1", "GW_1"):
        op("v", [], [reg(b, 2048, 2064)], lambda: g.vector.memset(T[b][:, 2048:2064], 0.0))
    ts(("JB", 0, 128), ("IB", 0, 128), 4, AluOpType.arith_shift_right)
    ts(("JM", 0, 16), ("IM", 0, 16), 15, AluOpType.bitwise_and)
    ts(("BO", 0, 128), ("JB", 0, 128), 8, eq)
    ts(("MK", 0, 16), ("JM", 0, 16), 0, eq, 1.0 / 1024, mult)
    for c in range(16):
        o, m = ("BK", 128 * c, 128 * c + 128), reg("MK", c, c + 1)
        if c % 2:
            actv(o, ("BO", 0, 128), act.Identity, 0.0, T.MK[:, c:c + 1], [m])
        else:
            ts(o, ("BO", 0, 128), T.MK[:, c:c + 1], mult, None, None, [m])
    ts(("JW", 0, 256), ("IW", 0, 256), 127, AluOpType.bitwise_and)
    ts(("W", 0, 256), ("JW", 0, 256), 0, eq)
    ts(("NI", 0, 128), ("JW", 0, 128), 0, eq, -1, mult)
    ts(("I4", 0, 128), ("JW", 0, 128), 0, eq, 4, mult)

    for sem, a, b, buf, n in (("EE", "se", "le", "E32", 392), ("XX", "sx", "lx", "N0", S)):
        for r in [me] + order:
            t = a if r == me else b
            dma("y", T[buf][32 * r:32 * r + 32, 0:n], T[t][r], sem, 64, [reg(t, r, r + 1)], [reg(buf, 0, n, 32 * r, 32 * r + 32)])
    for r in [me] + order:
        t = "sl" if r == me else "ll"
        dma("g", T.CPL[32 * r:32 * r + 32, :], T[t][r], "gl", 64, [reg(t, r, r + 1)], [reg("CPL", 0, 588, 32 * r, 32 * r + 32)])
    copy("v", ("RB", 0, 98), ("E32", 196, 294))
    copy("v", ("LST", 0, 354), ("E32", 0, 354))

    def spread(p, p0, c0, c1):
        for c in range(c0, c1):
            a = p0 + 98 * (c - c0)
            mm((p, a, a + 98), ("BK", 128 * c, 128 * c + 128), ("RB", 0, 98), True, True)
    for k, p, p0, c0, c1 in (("s", "pa", 0, 4, 9), ("v", "pa", 512, 9, 13), ("s", "pb", 0, 13, 16)):
        spread(p, p0, c0, c1)
        copy(k, ("K", 98 * c0, 98 * c1), (p, p0, p0 + 98 * (c1 - c0)))

    RE, SP, RXL = 0, 294, 324

    def border(s, e, win, c0):
        se = "SE%d_%d" % (e, s)
        pick("v", (se, 224, 480), win, S, "LST", c0 + 14)
        pick("s", (se, 0, 224), win, S, "LST", c0)
        for m, k in ((2, "s"), (0, "v"), (1, "s")):
            mm(("pe%d" % m, 0, 160), ("W", 32 * (1 + m), 32 * (1 + m) + 128), (se, 160 * (2 - m), 160 * (3 - m)), True, True)
            copy(k, (win, S + 160 * m, S + 160 * m + 160), ("pe%d" % m, 0, 160))

    for s in range(2):
        def nm(b):
            return "%s_%d" % (b, s)
        NW, FW, UW, GW = "N%d" % s, nm("FW"), nm("UW"), nm("GW")
        border(s, 0, NW, SP)
        if s == 0:
            spread("pk", 0, 0, 5)

        def kx(i, h):
            a, n = AC[i]
            o, x = ((nm("TA"), a, a + n), ("K", a, a + n)) if h == 0 else ((nm("TP"), a, a + n), (nm("TA"), a, a + n))
            pickop(o, NW, 2048, "LST", RE + 98 * h + a // 16, x, mult)

        def whole(i, k):
            a, n = AC[i]
            p, fa, fb, f = [(b, a, a + n) for b in (nm("TP"), nm("FA"), nm("FB"), FW)]
            if k == "s":
                actv(fa, p, act.Identity, HALF, 1.0)
                actv(fb, fa, act.Relu, 132.0, -1.0)
                actv(f, fb, act.Identity, 3.0, -1.0)
            else:
                ts(fa, p, 3.4, amin, HALF, add)
                ts(f, fa, -129.0, add)
        n = AC[0][1]
        pick("s", (nm("X2"), 0, n), NW, 2048, "LST", RE + 98)
        mm(("pa", 0, n), EYE, (nm("X2"), 0, n), True, True)
        pick("s", (nm("X1"), 0, n), NW, 2048, "LST", RE)
        kx(1, 0)
        kx(1, 1)
        whole(1, "s")
        tt((nm("TA"), 0, n), ("pa", 0, n), (nm("X1"), 0, n), mult)
        tt((nm("TP"), 0, n), ("pk", 0, n), (nm("TA"), 0, n), mult)
        whole(0, "s")
        kx(2, 0)
        kx(2, 1)
        whole(2, "v")
        border(s, 1, FW, RXL)
        DB, DG = nm("DB"), nm("DG")
        A = 896
        D = [(0, 608, "pa"), (608, A - 608, "pb")]
        for a, n, p in D:
            for c in range(3):
                pick("s", (DG, S * c + a, S * c + a + n), FW, 2049, "CPL", 98 * c + a // 16)
                mmw(p, 0, EYE, DG, S * c + a, n, c == 0, c == 2)
        for c in range(3):
            pickop((DB, A, S), FW, 2049, "CPL", 98 * c + A // 16, (NW if c == 0 else DB, A, S), sub if c == 0 else add)
        ts((UW, A, S), (DB, A, S), 0.0, le)
        for a, n, p in D:
            tt((UW, a, a + n), (p, 0, n), (NW, a, a + n), le)
        border(s, 2, UW, SP)
        VT, VG = nm("VT"), nm("VG")
        A = 960
        mmw("pb", 0, EYE, FW, A, S - A, True, False)
        pick("s", (VG, A, S), UW, 2048, "LST", RE + A // 16)
        mmw("pb", 0, I4, VG, A, S - A, False, False)
        for a, n in ((A, 512), (A + 512, S - A - 512)):
            pick("s", (VG, S + a, S + a + n), UW, 2048, "LST", RE + 98 + a // 16)
            mmw("pb", a - A, I4, VG, S + a, n, False, True)
        for h in range(2):
            pickop((VT, 0, A) if h == 0 else (GW, 0, A), UW, 2048, "LST", RE + 98 * h, (FW, 0, A) if h == 0 else (VT, 0, A), mult)
        for a, n in ((A, 512), (A + 512, S - A - 512)):
            actv((GW, a, a + n), ("pb", a - A, a - A + n), act.Relu, -8.0, 1.0)
        border(s, 3, GW, RXL)
        UA, UG = nm("UA"), nm("UG")
        out = "N1" if s == 0 else "ON"

        def uv(a, n, j):
            acc = (UA, a, a + n)
            pickop((out, a, a + n) if j == 5 else acc, GW, 2049, "CPL", 98 * j + a // 16,
                   (NW, a, a + n) if j == 0 else acc, sub if j in (0, 3) else add)

        def us(a, n, j, p0):
            pick("s", (UG, S * j + a, S * j + a + n), GW, 2049, "CPL", 98 * j + a // 16)
            mmw("pa", p0, NEG if j < 3 else EYE, UG, S * j + a, n, j == 0, j == 5)

        def fin(a, n, p0):
            tt((out, a, a + n), ("pa", p0, p0 + n), (NW, a, a + n), add)

        def ship(i):
            a, n = CO[i]
            dma("y", T["so%d" % i][:], T.ON[:, a:a + n], "o%d" % i, 16, [reg("ON", a, a + n)], [reg("so%d" % i, 0, 4)])
        if s == 0:
            for j in range(5):
                us(0, 800, j, 0)
            us(0, 512, 5, 0)
            us(512, 288, 5, 512)
            for j in range(6):
                uv(800, 768, j)
            fin(0, 512, 0)
            fin(512, 288, 512)
        else:
            for j in range(6):
                us(0, 512, j, 0)
            for j in range(6):
                us(992, 288, j, 512)
            for j in range(6):
                uv(512, 480, j)
            uv(1280, 288, 0)
            fin(0, 512, 0)
            ship(0)
            for j in range(1, 6):
                uv(1280, 288, j)
            fin(992, 288, 512)
            ship(1)

    mine = slice(32 * me, 32 * me + 32)
    parts = [(lo, hi) for lo, hi in ((0, me), (me + 1, N)) if lo < hi]
    full = 16 * (2 + len(parts))

    def own(i):
        a, n = CO[i]
        dma("g", T.y[mine, a:a + n], T.ON[mine, a:a + n], "gy", full, [reg("ON", a, a + n)], [])

    def slot(r, q):
        i = [c for c in range(N) if c != r].index(q)
        return LW * i, LW * i + LW
    own(0)
    send("so0", lambda r: T.ly0[me], "ay0", [reg("so0", 0, 4)])
    arrives("ay0", [reg("ly0", r, r + 1) for r in others], others)
    own(1)
    send("so1", lambda r: T.LY[:, slot(r, me)[0]:slot(r, me)[1]], "ay1", [reg("so1", 0, 4)])
    arrives("ay1", [reg("LY", 0, 3 * LW)], others)
    a, n = CO[0]
    for lo, hi in parts:
        dma("g", T.y[32 * lo:32 * hi, a:a + n], T.ly0[lo:hi], "gy", full, [reg("ly0", lo, hi)], [])
    copy("v", ("LF", 0, 3 * LW), ("LY", 0, 3 * LW))
    a, n = CO[1]
    for i, r in enumerate(others):
        dma("s" if i == 1 else "y", T.y[32 * r:32 * r + 32, a:a + n], T.LF[:, LW * i:LW * i + LW], "yy", 48,
            [reg("LF", LW * i, LW * i + LW)], [])
    for sem in total:
        if waited.get(sem, 0) < total[sem]:
            g.wait_ge(T.sem[sem], total[sem])
